import numpy as np, ml_dtypes
CORES = [36,164,52,180,100,228,116,244]
N = 8
BF = ml_dtypes.bfloat16
W, A, S, RO, H = 4096, 256, 2, 4, 3
def parts(rng):
    z = rng.integers(0, 256, (N, 8, 16, W)); w = rng.integers(0, 256, (N, 8, 16, 3)); w[..., 2] = rng.integers(0, 2048, (N, 8, 16))
    return z, w, rng.choice(np.array([750, 850, 950, 1200]), (N, 8, 1, 1))
def loose(rng):
    share = rng.choice(np.array([0.06, 0.15, 0.4, 0.9]), (N, 8, 1, A))
    return np.where(rng.random((N, 8, 16, A)) < share, rng.integers(0, W, (N, 8, 16, A)), -1)
def objects(rng, z, n):
    ix = np.argsort(rng.random((N, 8, W)), axis=-1)[..., :S * 2 * n]
    base = rng.integers(40, 216, (8, 16, 1, 1, n)); dev = rng.integers(-16, 17, (8, 16, 16, 2, n))
    order = np.argsort(rng.random((8, 16, n)), axis=1); rows = np.arange(16)[None, :, None]
    up = rows == order[:, :1]; down = rows == order[:, 1:2]
    v = base + np.where(up[:, None, :, None, :], 16, np.where(down[:, None, :, None, :], -16, dev))
    for q in range(N):
        np.put_along_axis(z[q], np.broadcast_to(ix[q][:, None, :], (8, 16, S * 2 * n)), v[:, :, S * q:S * q + S].reshape(8, 16, S * 2 * n), 2)
    return np.ascontiguousarray(ix.reshape(N, 8, S, 2, n).transpose(1, 0, 2, 3, 4)).reshape(8, 16, 2, n), up | down
def follow(rng, obj, am):
    out = []
    for r in range(N):
        c = rng.integers(0, obj.shape[-1], (8, 1, A))
        one = np.take_along_axis(obj[:, :, 0], c, 2); two = np.take_along_axis(obj[:, :, 1], c, 2); anchor = np.take_along_axis(am, c, 2)
        v = (rng.random((8, 16, A)) < rng.choice(np.array([0, 0, 0.1, 0.5]), (8, 1, A))) & ~anchor
        keep = anchor | (rng.random((8, 16, A)) < rng.random((8, 1, A)))
        out.append(np.where(keep, np.where(v, two, one), -1))
    return np.stack(out)
def pack(z, w, t, p, s):
    return {"tz": np.ascontiguousarray(z.reshape(N, 128, W)).astype(np.float32).astype(BF), "tp": np.ascontiguousarray(p.reshape(N, 128, A)).astype(np.int32),
            "sd": np.ascontiguousarray(s.reshape(N, 128, A)).astype(np.int32), "hw": np.ascontiguousarray(w.reshape(N, 128, 3)).astype(np.int32),
            "th": np.repeat(t.reshape(N, 8, 1), 16, axis=1).astype(np.int32)}
def setup_inputs(rng):
    z, w, t = parts(rng); obj, am = objects(rng, z, A // 4)
    p = np.where(rng.random((N, 8, 1, A)) < 0.5, follow(rng, obj, am), loose(rng))
    s = np.where(rng.random((N, 8, 1, A)) < 0.5, follow(rng, obj, am), loose(rng))
    return pack(z, w, t, p, s)
def setup_inputs_twins(rng):
    z, w, t = parts(rng); obj, am = objects(rng, z, 4); t[:] = 4096
    p = follow(rng, obj, am); p[:, 6:] = loose(rng)[:, 6:]; p[..., A // 2:] = p[..., :A // 2].copy()
    return pack(z, w, t, p, follow(rng, obj, am))
def setup_inputs_ties(rng):
    z, w, t = parts(rng)
    z = np.take_along_axis(rng.integers(0, 256, (N, 8, 16, 6)), rng.integers(0, 6, (N, 8, 1, W)), 3)
    t = rng.choice(np.array([1000, 4096]), (N, 8, 1, 1)); p = loose(rng); s = loose(rng)
    w[:, 0, :, :2] = 0; w[:, 1, :, 2] = 0; w[:, 4, :, 2] = rng.choice(np.array([5, 1031]), (N, 16)); t[:, :2] = 4096
    z[:, 2:4] = 100; t[::2, 2] = 0; t[1::2, 2] = 1; t[:, 3] = 432; p[:, 2:4, :, ::4] = -1
    return pack(z, w, t, p, s)
def setup_inputs_ends(rng):
    z = 255 * rng.integers(0, 2, (N, 8, 16, W)); ends = np.array([-1, 0, 1, W - 2, W - 1])
    p = rng.choice(ends, (N, 8, 16, A)); s = rng.choice(ends, (N, 8, 16, A)); t = rng.choice(np.array([0, 1, 2040, 4080, 4096]), (N, 8, 1, 1))
    w = rng.choice(np.array([0, 1, 254, 255]), (N, 8, 16, 3)); w[..., 2] = rng.choice(np.array([0, 1, 1025, 2046, 2047]), (N, 8, 16))
    p[:, 4] = rng.integers(0, W, (N, 16, A)); t[:, 4] = 4096
    z[:, 5] = 255; w[:, 5, :, :2] = 0; w[:, 5, 0, :2] = 255; w[:, 5, 1, :2] = 2; w[:, 5, :, 2] = 2047; t[:, 5] = 4096
    p[:, 6] = -1; t[:, 6] = 4096
    z[::2, 7] = 255; z[1::2, 7] = 0; p[:, 7] = rng.integers(0, W, (N, 16, A)); p[:, 7, (np.arange(16) // S) % 2 == 1] = -1
    t[1::4, 7] = 4081; t[3::4, 7] = 4080
    w[1::2, 7, :, 0] = 0; w[1::2, 7, :, 1] = 254 * rng.integers(0, 2, (N // 2, 16)); w[1::2, 7, 0, 1] = 255; w[1::2, 7, 0, 2] = rng.integers(1, 2048, N // 2)
    return pack(z, w, t, p, s)
def setup_inputs_sparse(rng):
    z, w, t = parts(rng); t = rng.choice(np.array([900, 4096]), (N, 8, 1, 1)); t[:, 0] = 4096
    p = np.where(rng.random((N, 8, 16, A)) < 0.06, rng.integers(0, W, (N, 8, 16, A)), -1); p[rng.integers(0, N)] = -1
    s = loose(rng); s[:, rng.permutation(8)[:4]] = -1
    return pack(z, w, t, p, s)
def setup_inputs_spread(rng):
    z = np.minimum((np.exp2(8.0 * rng.random((N, 8, 1, W))) * rng.random((N, 8, 16, W))).astype(np.int64), 255)
    w = np.minimum(np.exp2(8.0 * rng.random((N, 8, 16, 3))).astype(np.int64), 255); w[..., 2] = np.minimum(np.exp2(11.0 * rng.random((N, 8, 16))).astype(np.int64), 2047)
    t = np.minimum(np.exp2(7.0 + 5.0 * rng.random((N, 8, 1, 1))).astype(np.int64), 4096)
    ps = []
    for i in range(2):
        nm = np.minimum((W * rng.random((N, 8, 16, A)) ** 3).astype(np.int64), W - 1)
        ps.append(np.where(rng.random((N, 8, 16, A)) < rng.random((N, 8, 1, A)), nm, -1))
    return pack(z, w, t, ps[0], ps[1])
def check_inputs(d):
    bad = []; v = np.asarray(d["tz"]).astype(np.float32)
    if not (np.min(v) >= 0 and np.max(v) <= 255 and np.all(v == np.floor(v))): bad.append("tz: whole numbers from 0 to 255")
    for k, lo, hi in (("tp", -1, W - 1), ("sd", -1, W - 1), ("th", 0, 4096)):
        if np.min(d[k]) < lo or np.max(d[k]) > hi: bad.append("range of " + k)
    w = np.asarray(d["hw"])
    if np.min(w) < 0 or np.max(w[..., :2]) > 255 or np.max(w[..., 2]) > 2047: bad.append("range of hw")
    t = np.asarray(d["th"]).reshape(-1, 16)
    if np.any(t != t[:, :1]): bad.append("th: one number a group")
    return bad
def reference(tz, tp, sd, hw, th):
    z = tz.astype(np.float32).astype(np.int32).reshape(N, 8, 16, W); w = hw.astype(np.int32).reshape(N, 8, 16, 3); lim = th.astype(np.int32).reshape(N, 8, 16)[:, :, :1]
    p = tp.astype(np.int32).reshape(N, 8, 16, A); s = sd.astype(np.int32).reshape(N, 8, 16, A); lower = np.arange(A)[None, :] < np.arange(A)[:, None]
    for t in range(RO):
        for r in range(N):
            q = (r + 1 + t) % N; x = S * q + t // N
            hi = np.zeros((8, 16, A), np.int32); lo = np.full((8, 16, A), 255, np.int32)
            for j in range(16):
                n = p[r, :, j]; on = (n >= 0)[:, None, :]; v = np.take_along_axis(z[j // S], np.maximum(n, 0)[:, None, :], 2)
                hi = np.where(on, np.maximum(hi, v), hi); lo = np.where(on, np.minimum(lo, v), lo)
            e = (hi + lo) >> 1; c = e
            best = np.full((8, A), 4097); name = np.zeros((8, A), np.int64)
            for k in range(H):
                u1 = np.add.reduce(w[q, :, :, 0:1] * c, axis=1) & (W - 1); u2 = np.add.reduce(w[q, :, :, 1:2] * c, axis=1) & (W - 1)
                h = (((u1 * u2) >> 5)[:, None, :] + w[q, :, :, 2:3] * u2[:, None, :]) & (W - 1)
                v = np.take_along_axis(z[q], h.reshape(8, 1, 16 * A), 2).reshape(8, 16, 16, A)
                d = np.add.reduce(np.abs(v - e[:, :, None, :]), axis=1)
                m = np.argmin(d, axis=1); dm = np.min(d, axis=1); n = np.take_along_axis(h, m[:, None, :], 1)[:, 0]
                less = dm < best; name = np.where(less, n, name); best = np.where(less, dm, best)
                c = (e + np.take_along_axis(z[q], n[:, None, :], 2)) >> 1
            n = np.where(best < lim[q], name, -1); p[r, :, x] = n
            low = (n[:, :, None] == n[:, None, :]) & (n >= 0)[:, :, None] & lower
            g, b = np.nonzero(np.count_nonzero(low, axis=2) == 1); a = np.argmax(low[g, b], axis=1)
            pa = p[r][g, :, a]; pb = p[r][g, :, b]; differ = (pa >= 0) & (pb >= 0) & (pa != pb); clash = np.any(differ, axis=1)[:, None]
            p[r][g, :, a] = np.where(clash, np.where(differ, -1, pa), np.where(pa >= 0, pa, pb))
            p[r][g, :, b] = np.where(clash, np.where(differ, -1, pb), s[r][g, :, b])
    return {"yp": p.reshape(N, 128, A).astype(np.float32)}

from concourse.bass import DstId, RemoteDMATransfer
from concourse.mybir import AluOpType as OP, AxisListType, ActivationFunctionType as AF

BLK = 4112
KV, KC = 80, 32
EV = (1, 3)
BIG = 16777216.0
LAT = 0.1
F32, BF, I32, U16, F16 = "float32", "bfloat16", "int32", "uint16", "float16"

SCRATCH = {"TW": ("sbuf", [128, 8 * BLK], BF), "D": ("dram", [8, 128, 32], I32)}
WIDTH, PLACE, _used = {"TW": 8 * BLK, "D": 1}, {}, {}
for _n, _w, _d in (("NL", 256, I32), ("HT", 4, I32), ("HS", 16, I32), ("FO", 4096, BF), ("FI", 4096, BF), ("P", 512, F32), ("TP", 256, I32), ("SD", 256, I32), ("YO", 256, F32)):
    SCRATCH[_n], WIDTH[_n] = ("sbuf", [128, _w], _d), _w
for _k in range(8):
    SCRATCH["B%d" % _k], WIDTH["B%d" % _k] = ("psum", [128, 512], F32), 512
SPEC = ((BF, 1, "FA 2048 FB 2048 HI 2048 LO 2048 ER 2048 XV 2048 AX 2048 EB 128"), (F16, 1, "HB 16 HX 128 C 128"), (U16, 1, "OF 128 JU 16 L1U 8 L2U 8"),
        (F32, 1, "SE 128 E2 128 SC 128 LT 128 VAL 8 M1 8 M2 8 GG 128 PR 128 PK 128"),
        (I32, 1, "EI 128 UI 16 UA 16 VP 8 HN 128 KI 8 J 8 R 24 I1 128 I2 128 BA 8 BK 8 PI 8 L1 8 MI 8"),
        (F32, 0, "Y1 16 Y2 16 SEC 16 DD 16 DS 16 LF 16 EE 16 LSF 16 SN 256 Q 256 MN 256 QN 256 SP 256 SPS 256 SX 256 PC 256 S 256 HF 16 cone 512 cid 128 "
                 "cb1 128 cblk 128 cg1 8 cg 8 cmi 128 cmk 128 cm0 128 cj 1 cq 1 cs 1 cn 1 cpar 1 cnpar 1 ceb 1 clb 1 cba 16 cb2 16 cbf 16 cio 256 ci2 256 "
                 "clc 256 cth 512 cw0f 16 coh 32 cohi 32 cbt 16 csc 1 cc 8 cnegf 128 ntx 4 XM 128 XS 512 th 4 hcol 4 WF 64 cbm0 128"),
        (I32, 0, "HST 1024 cpi 1 cpj 1 cpq 1 cpt 1 cbai 16 cpc 24 cR 24 kd 16"),
        (BF, 0, "BE 256 BO 256 QA 1024 QX 1024 QB 1024 ND 256 cib 128 cnb 128 cblb 128 cgk 8 cmh 512 cml 512 WB 64"),
        (U16, 0, "NO 256 EO 256 LC 256 LU 16 LSU 16"), (F16, 0, "cw0 16 cw1 16 cneg 128 cih 128 cbm 128 WH 64 ZZ 64 KM 512"))
ARENA = {F32: "af", BF: "ab", I32: "ai", U16: "au", F16: "ah"}
for _d, _half, _s in SPEC:
    _it = _s.split()
    for _n, _w in zip(_it[::2], _it[1::2]):
        for _t in (("_0", "_1") if _half else ("",)):
            _a, _step = ARENA[_d], 16 if _d in (F32, I32) else 32
            PLACE[_n + _t], WIDTH[_n + _t] = (_a, _used.get(_a, 0)), int(_w)
            _used[_a] = _used.get(_a, 0) - (-int(_w) // _step) * _step
for _d in ARENA:
    SCRATCH[ARENA[_d]] = ("sbuf", [128, _used[ARENA[_d]]], _d)
SEMAPHORES = ["qv", "qs", "qt", "qg", "stg", "dtz", "dhw", "dtp", "dsd", "dnl", "dyp", "nm", "hs", "ft", "tb0", "tbx", "rel", "loc"]


def helper_of(rc, T, topo):
    for c in topo.cores_of(rc):
        if topo.die(c) != topo.die(rc) and c not in T.cores and all(topo.may_write(c, d) for d in T.cores if d != rc):
            return c
    return None


def send(g, T, topo, core, dst, out, in_, rsem, engines=None):
    rid, pid = topo.addr(dst, core)
    eng = topo.engines(core, dst) if engines is None else engines
    m = 0
    for e in eng:
        m |= 1 << e
    g.remote_dma(out, in_, T.sem[rsem], T.sem.loc, pid, rid, m)
    return len(eng)


def relay_engines(rc, hc, topo, T):
    off = topo.engines(rc, T.cores[0] if T.cores[0] != rc else T.cores[1])
    e = [x for x in topo.engines(rc, hc) if x not in off]
    return e if len(e) in (1, 2, 4, 8, 16) else topo.engines(rc, hc)


def rank_program(g, core, T, topo):
    N = len(T.cores)
    r = T.rank_of(core)
    if r is not None:
        main(g, core, T, topo, r, N)
        return
    for s in range(N):
        if helper_of(T.cores[s], T, topo) == core:
            blk = T.TW[:, BLK * s + 16:BLK * (s + 1)]
            g.wait_ge(T.sem.rel, len(relay_engines(T.cores[s], core, topo, T)))
            tot = 0
            for o in (1, 2, 4, 6):
                tot += send(g, T, topo, core, T.cores[(s - o) % N], blk, blk, "tb0" if o == 1 else "tbx")
            g.wait_ge(T.sem.loc, tot)


def is_bank(n):
    return n[0] == "B" and n[1:].isdigit()


def overlap(x, y):
    if x[1] >= y[2] or y[1] >= x[2] or x[3] >= y[4] or y[3] >= x[4]:
        return False
    return not (x[5] == y[5] and x[5] > 1 and (x[3] - y[3]) % x[5])


def covers(x, y):
    return x[5] == 1 and x[1] <= y[1] and x[2] >= y[2] and x[3] <= y[3] and x[4] >= y[4]


def schedule(ops):
    n = len(ops)
    preds, succs, acc, lastg = [set() for _ in ops], [[] for _ in ops], {}, None
    for i, (q, rd, wr, _, _, _) in enumerate(ops):
        if q == "g":
            if lastg is not None:
                preds[i].add(lastg)
            lastg = i
        for keys, w in ((rd, False), (wr, True)):
            for x in keys:
                lst = acc.setdefault(x[0], [])
                if is_bank(x[0]):
                    preds[i].update(e[2] for e in lst)
                    acc[x[0]] = [(x, True, i)]
                    continue
                preds[i].update(e[2] for e in lst if (w or e[1]) and overlap(x, e[0]))
                acc[x[0]] = [e for e in lst if not (w and covers(x, e[0]))] + [(x, w, i)]
        preds[i].discard(i)
    for i in range(n):
        for j in preds[i]:
            succs[j].append(i)
    prio = [0.0] * n
    for i in range(n - 1, -1, -1):
        prio[i] = ops[i][4] + max([prio[j] + LAT for j in succs[i]] + [0.0])
    left = [len(p) for p in preds]
    start, fin, free = [0.0] * n, [0.0] * n, {}
    ready = {i: ops[i][5] for i in range(n) if not left[i]}
    while ready:
        t0, _, i = min((max(ready[i], free.get(ops[i][0], 0.0)), -prio[i], i) for i in ready)
        del ready[i]
        q = ops[i][0]
        start[i], fin[i] = t0, t0 + ops[i][4]
        if q != "x":
            free[q] = fin[i]
        for j in succs[i]:
            left[j] -= 1
            if not left[j]:
                ready[j] = max([ops[j][5]] + [fin[k] + (0.0 if ops[k][0] == "t" == ops[j][0] else LAT) for k in preds[j]])
    return [ops[i] for i in sorted(range(n), key=lambda i: (start[i], i))]


def main(g, core, T, topo, r, N):
    eng = {"v": g.vector, "s": g.scalar, "t": g.tensor, "g": g, "y": g.sync}
    qsem = {"v": "qv", "s": "qs", "t": "qt", "g": "qg"}
    cnt = {"v": 0, "s": 0, "t": 0, "g": 0}
    known = {q: {} for q in eng}
    snaps, acc, ops = {}, {}, []

    def need(q, sem, val):
        k = known[q]
        if k.get(sem, 0) >= val:
            return
        eng[q].wait_ge(T.sem[sem], val)
        for s, v in snaps.get((sem, val), {}).items():
            if k.get(s, 0) < v:
                k[s] = v
        k[sem] = val

    def order(q, reads, writes):
        todo = {}
        for keys, w in ((reads, False), (writes, True)):
            for x in keys:
                keep = []
                for e in acc.get(x[0], []):
                    y, ew, eq, sem, val = e
                    if is_bank(x[0]):
                        hit = eq != q or ((ew or w) and overlap(x, y) if q != "t" else x[6:] != y[6:])
                        drop = eq != q
                    else:
                        hit = (ew or w) and overlap(x, y)
                        drop = w and covers(x, y)
                    if hit and todo.get(sem, 0) < val:
                        todo[sem] = val
                    if not drop:
                        keep.append(e)
                acc[x[0]] = keep
        for sem in sorted(todo, key=lambda s: (s == qsem.get(q), s)):
            need(q, sem, todo[sem])

    def note(q, reads, writes, sem, val):
        for keys, w in ((reads, False), (writes, True)):
            for x in keys:
                lst = acc.setdefault(x[0], [])
                lst[:] = [e for e in lst if not (e[0] == x and e[1] == w and e[2] == q and e[3] == sem)]
                lst.append((x, w, q, sem, val))
        snaps[(sem, val)] = dict(known.get(q, {}))

    def rec(q, rd, wr, call, cost):
        def emit():
            order(q, rd, wr)
            i = call()
            if i is not None:
                cnt[q] += 1
                i.then_inc(T.sem[qsem[q]], 1)
                note(q, rd, wr, qsem[q], cnt[q])
        ops.append([q, rd, wr, emit, cost, 0.0])

    def ext(writes, sem, val, when):
        ops.append(["x", [], writes, lambda: note("ext", [], writes, sem, val), 0.01, when])

    def A(n, c0=0, c1=None, st=1, p0=0, p1=128):
        c1 = WIDTH[n] if c1 is None else c1
        b, o = PLACE.get(n, (n, 0))
        return (T[b][p0:p1, o + c0:o + c1] if st == 1 else T[b][p0:p1, o + c0:o + c1:st], [(n, p0, p1, c0, c1, st)], -(-(c1 - c0) // st))

    def IND(w, o):
        return (w[0].indirect(o[0]), w[1] + o[1], 16 * o[2], True)

    def vcost(out, ins, per):
        if any(len(o) > 3 for o in [out] + ins):
            return 0.05 + 0.0015 * (2.5 if len(out) > 3 else 1) * out[2]
        return 0.064 * max(1.0, per * out[2] / 64.0)

    def copy(out, in_):
        rec("v", in_[1], out[1], lambda: g.vector.tensor_copy(out[0], in_[0]), vcost(out, [in_], 1))

    def tt(out, a, b, o):
        wr, rd = out[1], a[1] + b[1]
        if len(out) > 3:
            wr, rd = out[1][:1], rd + out[1]
        two = not (is_bank(a[1][0][0]) or is_bank(b[1][0][0]))
        rec("v", rd, wr, lambda: g.vector.tensor_tensor(out[0], a[0], b[0], o), vcost(out, [a, b], 2 if two else 1))

    def ts(out, a, s1, s2, o1, o2=None):
        rd = a[1] + [k for s in (s1, s2) if isinstance(s, tuple) for k in s[1]]
        v1 = s1[0] if isinstance(s1, tuple) else s1
        v2 = s2[0] if isinstance(s2, tuple) else s2
        if o2 is None:
            rec("v", rd, out[1], lambda: g.vector.tensor_scalar(out[0], a[0], v1, v2, o1), vcost(out, [a], 1))
        else:
            rec("v", rd, out[1], lambda: g.vector.tensor_scalar(out[0], a[0], v1, v2, o1, o2), vcost(out, [a], 1))

    def scan(out, d0, d1, init, o1, o2, per=1):
        rec("v", d0[1] + d1[1], out[1], lambda: g.vector.tensor_tensor_scan(out[0], d0[0], d1[0], init, o1, o2), vcost(out, [], per))

    def act(out, in_, f, bias=None):
        c = 0.065 + 0.0015 * out[2] if len(in_) > 3 else 0.064 * max(1.0, out[2] / 64.0)
        if bias is None:
            rec("s", in_[1], out[1], lambda: g.scalar.activation(out[0], in_[0], f), c)
        else:
            rec("s", in_[1], out[1], lambda: g.scalar.activation(out[0], in_[0], f, bias=bias), c)

    def mm(out, l, rh, start=True, stop=True, f32=False):
        rec("t", l[1] + rh[1], [out[1][0] + l[1][0][1:3]], lambda: g.tensor.matmul(out[0], l[0], rh[0], start, stop), 0.001 * max(64, out[2]) * (4 if f32 else 1))

    def ms(out, c):
        rec("v", [], out[1], lambda: g.vector.memset(out[0], c), vcost(out, [], 1))

    def iota(out, pat, base, cm, exact=False):
        if exact:
            rec("g", [], out[1], lambda: g.iota(out[0], pat, base, cm), 0.15 + 0.002 * out[2])
        else:
            rec("g", [], out[1], lambda: g.iota(out[0], pat, base, cm, allow_small_or_imprecise_dtypes=True), 0.15 + 0.002 * out[2])

    def asel(out, in_, pat, cmp, fill, base, cm):
        rec("g", in_[1], out[1], lambda: g.affine_select(out[0], in_[0], pat, cmp, fill, base, cm), 0.2 + 0.002 * out[2])

    def remote(rd, f):
        rec("g", rd, [], lambda: f(), 1.0)

    hc = helper_of(core, T, topo)
    qs = [(r + 1 + t) % N for t in range(4)]
    others = [d for d in range(N) if d != r]
    dkey = [("D", 0, 128, 0, 1, 1)]
    own = A("TW", BLK * r + 16, BLK * (r + 1))
    tot_loc = [0]

    for k in range(8):
        (g.sync if k % 2 == 0 else g.scalar).dma_start(T.D[:, 16 * k:16 * k + 16, :], T.tp[16 * k:16 * k + 16, :]).then_inc(T.sem.stg, 16)
    g.scalar.dma_start(T.HT[:, 0:3], T.hw[:]).then_inc(T.sem.dhw, 16)
    g.scalar.dma_start(T.HT[:, 3:4], T.th[:]).then_inc(T.sem.dhw, 16)
    g.sync.dma_start(own[0], T.tz[:]).then_inc(T.sem.dtz, 16)
    g.scalar.dma_start(T.TP[:], T.tp[:]).then_inc(T.sem.dtp, 16)
    g.scalar.dma_start(T.SD[:], T.sd[:]).then_inc(T.sem.dsd, 16)
    need("y", "stg", 128)
    g.sync.dma_start(T.NL[:, 32 * r:32 * r + 32], T.D[r]).then_inc(T.sem.dnl, 16)
    for k, sem, val, when in ((dkey, "stg", 128, 4.0), (A("HT")[1], "dhw", 32, 3.0), (own[1], "dtz", 16, 7.0), (A("TP")[1], "dtp", 16, 5.0),
                              (A("SD")[1], "dsd", 16, 6.0), (A("NL", 32 * r, 32 * r + 32)[1], "dnl", 16, 7.0)):
        ext(k, sem, val, when)

    for q in range(N):
        ms(A("TW", BLK * q, BLK * q + 16), -256.0)
    ms(A("cone"), 1.0)
    iota(A("cpi"), [[0, 1]], 0, 1, True)
    iota(A("cmi"), [[0, 8], [1, 16]], 0, 0)
    iota(A("clc"), [[1, 8], [16, 32]], 0, 0)
    iota(A("cbf"), [[16, 16]], 0, 0)
    asel(A("cid"), A("cone", 0, 128), [[-1, 128]], OP.is_equal, 0.0, 0, 1)

    def fused(pairs, rsem):
        tr = []
        for i, (d, src, dst) in enumerate(pairs):
            rid, pid = topo.addr(T.cores[d], core)
            e = topo.engines(core, T.cores[d])
            tr.append(RemoteDMATransfer(dst_ids=[DstId(rid=rid, pnc=pid)], dma_engine_mask=1 << e[i % len(e)], remote_sem=T.sem[rsem], srcs=[src], dsts=[dst]))
        g.remote_dma_fused(tr, local_sem=T.sem.loc)
        tot_loc[0] += len(tr)

    def table_out(d, rsem, engines=None):
        tot_loc[0] += send(g, T, topo, core, d, own[0], own[0], rsem, engines)

    remote(dkey, lambda: fused([(d, T.D[d], T.NL[:, 32 * r:32 * r + 32]) for d in others], "nm"))
    remote(A("HT")[1], lambda: fused([((r - 1 - t) % N, T.HT[:], T.HS[:, 4 * t:4 * t + 4]) for t in range(4)], "hs"))
    for d in others:
        ext(A("NL", 32 * d, 32 * d + 32)[1], "nm", N - 1, 8.0)
    ext(A("HS")[1], "hs", 4, 9.0)
    remote(own[1], lambda: table_out(hc, "rel", relay_engines(core, hc, topo, T)))
    asel(A("cb1"), A("cone", 0, 128), [[-16, 8], [0, 16]], OP.is_ge, 0.0, 0, 1)
    asel(A("cblk"), A("cb1"), [[16, 8], [0, 16]], OP.is_ge, 0.0, 15, -1)
    asel(A("cg1"), A("cone", 0, 8), [[-16, 8]], OP.is_ge, 0.0, 0, 1)
    asel(A("cg"), A("cg1"), [[16, 8]], OP.is_ge, 0.0, 15, -1)
    iota(A("cbm0"), [[0, 8], [1, 16]], 0, 16)
    iota(A("cohi"), [[1, 32]], 0, 0)
    iota(A("cw0f"), [[0, 16]], 256, 1)
    iota(A("cpc"), [[16, 3], [-256, 8]], 0, 0, True)
    ts(A("NO"), A("NL"), 16.0, None, OP.add)
    win = A("TW", BLK * r, BLK * (r + 1))
    for i, d in enumerate(others + [r]):
        o, a = A("FO", 512 * d, 512 * d + 512), IND(win, A("NO", 32 * d, 32 * d + 32))
        if i % 2:
            copy(o, a)
        else:
            act(o, a, AF.Copy)
    remote(A("FO", 0, 512 * r)[1] + A("FO", 512 * r + 512, 4096)[1],
           lambda: fused([(d, T.FO[:, 512 * d:512 * d + 512], T.FI[:, 512 * r:512 * r + 512]) for d in others], "ft"))
    act(A("FI", 512 * r, 512 * r + 512), A("FO", 512 * r, 512 * r + 512), AF.Copy)
    for d in others:
        ext(A("FI", 512 * d, 512 * d + 512)[1], "ft", N - 1, 20.0)
    for o in (3, 5, 7):
        remote(own[1], lambda o=o: table_out(T.cores[(r - o) % N], "tbx"))
    for q in others:
        ext(A("TW", BLK * q + 16, BLK * (q + 1))[1], *(("tb0", 8, 24.0) if q == qs[0] else ("tbx", 48, 60.0)))
    iota(A("cio"), [[1, 256]], 0, 0)
    iota(A("ci2"), [[1, 256]], 0, 0)
    ms(A("cth"), 14.0)
    asel(A("cth"), A("cth"), [[0, 4], [1, 128]], OP.is_gt, 1000.0, 0, -1)

    ts(A("cpj"), A("cpi"), 15, None, OP.bitwise_and)
    ts(A("cpq"), A("cpj"), 1, None, OP.arith_shift_right)
    ts(A("cpt"), A("cpi"), 4, 1, OP.arith_shift_right, OP.bitwise_and)
    copy(A("cj"), A("cpj"))
    copy(A("cq"), A("cpq"))
    copy(A("cpar"), A("cpt"))
    ts(A("cn"), A("cj"), -16.0, None, OP.mult)
    ts(A("cR"), A("cpc"), A("cn"), None, OP.add)
    ts(A("ceb"), A("cq"), float(BLK), 15.0, OP.mult, OP.add)
    ts(A("cs"), A("cq"), 496.0, None, OP.mult)
    ts(A("clb"), A("cj"), 8.0, A("cs"), OP.mult, OP.add)
    ts(A("LC"), A("clc"), A("clb"), None, OP.add)
    ts(A("cba"), A("cbf"), A("cj"), None, OP.add)
    ts(A("cbai"), A("cba"), 4.0, None, OP.mult)
    ts(A("cb2"), A("cba"), 256.0, None, OP.add)
    for n, fill, first in (("cmh", 256.0, 0.0), ("cml", 0.0, 255.0)):
        ms(A(n), fill)
        ms(A(n, 0, 512, 16), first)
    ms(A("cm0"), 0.0)
    ms(A("cm0", 0, 128, 16), BIG)
    ms(A("HST"), 0)
    ms(A("cnegf"), -2048.0)
    copy(A("cneg"), A("cnegf"))
    copy(A("cib"), A("cid"))
    copy(A("cih"), A("cid"))
    copy(A("cbm"), A("cbm0"))
    ts(A("cnb"), A("cid"), -1.0, None, OP.mult)
    copy(A("cblb"), A("cblk"))
    ts(A("cgk"), A("cg"), 2048.0, None, OP.mult)
    ts(A("cmk"), A("cmi"), A("cj"), None, OP.is_equal)
    ts(A("coh"), A("cohi"), A("cj"), None, OP.is_equal)
    copy(A("cw0"), A("cw0f"))
    ts(A("cw1"), A("cw0f"), 128.0, None, OP.add)
    copy(A("HF"), A("HS"))
    ts(A("kd"), A("HS"), 1, None, OP.bitwise_and)
    for t in range(4):
        for i in range(2):
            ts(A("WF", 16 * t + 8 * i, 16 * t + 8 * i + 8), A("cg"), A("HF", 4 * t + i, 4 * t + i + 1), None, OP.mult)
        copy(A("WB", 16 * t, 16 * t + 16), A("WF", 16 * t, 16 * t + 16))
        ts(A("WH", 16 * t, 16 * t + 16), A("WF", 16 * t, 16 * t + 16), 0.5, None, OP.mult)
        ts(A("th", t, t + 1), A("HF", 4 * t + 3, 4 * t + 4), 2048.0, None, OP.mult)
        ts(A("hcol", t, t + 1), A("kd", 4 * t + 2, 4 * t + 3), -2048.0, 4196352.0, OP.mult, OP.add)
        copy(A("ZZ", 16 * t, 16 * t + 8), A("cg"))
        ts(A("ZZ", 16 * t + 8, 16 * t + 16), A("cg"), A("HF", 4 * t + 2, 4 * t + 3), None, OP.mult)
        b = A("B%d" % (5 + t % 2), 0, 128, 1, 0, 16)
        mm(b, A("ZZ", 16 * t, 16 * t + 16), A("cih"))
        copy(A("KM", 128 * t, 128 * t + 128, 1, 0, 16), b)
        x = float(2 * qs[t] + t // N)
        ts(A("ntx", t, t + 1), A("cj"), x, None, OP.not_equal)
        ts(A("XM"), A("cmi"), x, None, OP.is_equal)
        tt(A("XS", 128 * t, 128 * t + 128), A("XM"), A("cblk"), OP.mult)
    ts(A("P", 0, 256), A("TP"), 1.0, None, OP.add)
    ts(A("S"), A("SD"), 1.0, None, OP.add)
    for j in range(16):
        ts(A("cbt", j, j + 1), A("cj"), float(j), float(2 ** (12 - j)) if j < 13 else (-1.0 if j == 13 else 0.0), OP.is_equal, OP.mult)
    rec("v", A("cbt")[1], A("csc")[1], lambda: g.vector.tensor_reduce(A("csc")[0], A("cbt")[0], AxisListType.X, OP.add), 0.07)
    ts(A("cnpar"), A("cpar"), -1.0, 1.0, OP.mult, OP.add)
    ts(A("cc", 4, 5), A("cj"), 13.0, 1.0 / 2048, OP.is_lt, OP.mult)
    ts(A("cc", 5, 6), A("cj"), 13.0, 1.0 / 4096, OP.is_equal, OP.mult)
    tt(A("cc", 6, 7), A("cc", 4, 5), A("cc", 5, 6), OP.add)
    ts(A("cc", 7, 8), A("cj"), 13.0, -1.0, OP.is_lt, OP.mult)
    for i, m in ((0, "cnpar"), (1, "cpar")):
        tt(A("cc", 2 * i, 2 * i + 1), A("cc", 6, 7), A(m), OP.mult)
        tt(A("cc", 2 * i + 1, 2 * i + 2), A("cc", 7, 8), A(m), OP.mult)

    def middle(h, t):
        s = "_%d" % h
        if t:
            ts(A("EO", 128 * h, 128 * h + 128), A("P", 128 * h, 128 * h + 128), A("ceb"), None, OP.add)
        for k in range(4):
            c, o = 512 * k, 128 * h + 32 * k
            src = IND(A("TW"), A("EO", o, o + 32)) if t else IND(A("FI"), A("LC", o, o + 32))
            if k in EV:
                copy(A("FA" + s, c, c + 512), src)
            else:
                act(A("FA" + s, c, c + 512), src, AF.Copy)
            act(A("FB" + s, c, c + 512), A("FA" + s, c, c + 512), AF.Abs)
            scan(A("HI" + s, c, c + 512), A("cmh"), A("FA" + s, c, c + 512), 0.0, OP.min, OP.max, 0.5)
            scan(A("LO" + s, c, c + 512), A("cml"), A("FB" + s, c, c + 512), 255.0, OP.max, OP.min, 0.5)
        tt(A("SE" + s), A("HI" + s, 15, 2048, 16), A("LO" + s, 15, 2048, 16), OP.add)
        ts(A("EI" + s), A("SE" + s), 0.5, -0.25, OP.mult, OP.add)
        copy(A("EB" + s), A("EI" + s))
        for m in range(16):
            if m % 8 < 5:
                copy(A("ER" + s, m, 2048, 16), A("EB" + s))
            else:
                act(A("ER" + s, m, 2048, 16), A("EB" + s), AF.Copy)
        ts(A("E2" + s, 0, KV), A("EI" + s, 0, KV), 2.0, 2047.5, OP.mult, OP.add)
        ts(A("E2" + s, KV, 128), A("EI" + s, KV, 128), 2047.5, None, OP.add)

    def hash_(h, p, t):
        s, b = "_%d" % h, "B%d" % (5 + h)
        u = A(b, 0, 16)
        if p == 0:
            mm(u, A("EB" + s), A("WB", 16 * t, 16 * t + 16))
        else:
            mm(u, A("cneg"), A("WH", 16 * t, 16 * t + 16), True, False)
            mm(u, A("C" + s), A("WH", 16 * t, 16 * t + 16), False, True)
        copy(A("UI" + s), u)
        ts(A("UA" + s), A("UI" + s), 4095, None, OP.bitwise_and)
        tt(A("VP" + s), A("UA" + s, 0, 8), A("UA" + s, 8, 16), OP.mult)
        ts(A("UA" + s, 0, 8), A("VP" + s), 5, 4095, OP.arith_shift_right, OP.bitwise_and)
        ts(A("HB" + s), A("UA" + s), -2048.0, None, OP.add)
        x, y = A(b, 16, 144, 1, 0, 16), A("HX" + s, 0, 128, 1, 0, 16)
        mm(x, A("HB" + s), A("cih"))
        copy(y, x)
        hh = A(b, 144, 272)
        mm(hh, A("KM", 128 * t, 128 * t + 128, 1, 0, 16), y)
        ts(A("HN" + s), hh, A("hcol", t, t + 1), None, OP.add)
        d = A("HST", 512 * h + p, 512 * h + 512, 4)
        ts(d, A("HN" + s), 4095, None, OP.bitwise_and)
        copy(A("OF" + s), d)

    def look(h, t):
        s, kb = "_%d" % h, "B%d" % (3 + h)
        w = A("TW", BLK * qs[t] + 16, BLK * qs[t] + BLK)
        mm(A(kb, 0, 128), A("cih"), A("cbm"), True, False)
        for c in range(0, KV, KC):
            x = (16 * c, 16 * min(KV, c + KC))
            tt(A("XV" + s, *x), IND(w, A("OF" + s, c, min(KV, c + KC))), A("ER" + s, *x), OP.subtract)
            act(A("AX" + s, *x), A("XV" + s, *x), AF.Abs)
        for i, c in enumerate(range(16 * KV, 2048, 512)):
            n = min(512, 2048 - c)
            b = A("B%d" % i, 0, n)
            act(A("XV" + s, c, c + n), IND(w, A("OF" + s, c // 16, (c + n) // 16)), AF.Copy)
            mm(b, A("cnb"), A("ER" + s, c, c + n), True, False)
            mm(b, A("cib"), A("XV" + s, c, c + n), False, True)
            act(A("AX" + s, c, c + n), b, AF.Abs)
        for m in range(16):
            mm(A(kb, m, 128, 16), A("AX" + s, m, 2048, 16), A("cgk"), False, m == 15)

    def winner(h, p):
        s = "_%d" % h
        scan(A("SC" + s), A("cm0"), A("B%d" % (3 + h), 0, 128), BIG, OP.max, OP.min)
        for k in range(8):
            ts(A("LT" + s, 16 * k, 16 * k + 16), A("cmk", 0, 16), A("SC" + s, 16 * k + 15, 16 * k + 16), None, OP.mult)
        sp = A("B%d" % (5 + h), 280, 288)
        mm(sp, A("LT" + s), A("cg"), f32=True)
        if p < 2:
            copy(A("KI" + s), sp)
            ts(A("J" + s), A("KI" + s), 2047, None, OP.bitwise_and)
            copy(A("JU" + s, 0, 8), A("J" + s))
            tt(A("C" + s), IND(A("XV" + s), A("JU" + s, 0, 8)), A("E2" + s), OP.add)
        tt(A("R" + s, 8 * p, 8 * p + 8), sp, A("cR", 8 * p, 8 * p + 8), OP.add)

    def names(h, t):
        s, c0, c1 = "_%d" % h, 128 * h, 128 * h + 128
        tt(A("BA" + s), A("R" + s, 0, 8), A("R" + s, 8, 16), OP.min)
        tt(A("BK" + s), A("BA" + s), A("R" + s, 16, 24), OP.min)
        ts(A("PI" + s), A("BK" + s), 4, 3, OP.arith_shift_right, OP.bitwise_and)
        ts(A("MI" + s), A("BK" + s), 15, None, OP.bitwise_and)
        ts(A("VAL" + s), A("BK" + s), A("th", t, t + 1), None, OP.is_lt)
        tt(A("L1" + s), A("PI" + s), A("cbai", 8 * h, 8 * h + 8), OP.add)
        ts(A("M1" + s), A("MI" + s), -16.0, None, OP.add)
        copy(A("L1U" + s), A("L1" + s))
        tt(A("M2" + s), A("M1" + s), A("VAL" + s), OP.mult)
        ts(A("L2U" + s), A("M2" + s), 16.0, None, OP.add)
        ts(A("GG" + s), IND(A("HST"), A("L1U" + s)), 1.0, 1.0, OP.mult, OP.add)
        tt(A("PR" + s), IND(A("coh"), A("L2U" + s)), A("GG" + s), OP.mult)
        nrep, nx = A("B7", c0, c1), A("B7", 256 + c0, 256 + c1)
        mm(nrep, A("cblk"), A("PR" + s), f32=True)
        mm(nx, A("XS", 128 * t, 128 * t + 128), A("PR" + s), f32=True)
        ts(A("I1" + s), nrep, A("csc"), None, OP.mult)
        ts(A("I2" + s), A("I1" + s), 4096, None, OP.bitwise_and)
        ts(A("BE", c0, c1), A("I2" + s), A("cc", 0, 1), A("cc", 1, 2), OP.mult, OP.add)
        ts(A("BO", c0, c1), A("I2" + s), A("cc", 2, 3), A("cc", 3, 4), OP.mult, OP.add)
        tt(A("B3", 128 + c0, 128 + c1), nx, A("PK" + s), OP.add)
        copy(A("P", c0, c1), A("B3", 128 + c0, 128 + c1))

    def pairs(t):
        ps = A("B3", 128, 384)
        for banks, a0, b0, out in (((0, 1), 0, 0, "QA"), ((2, 4), 0, 128, "QX"), ((5, 6), 128, 128, "QB")):
            for k in (0, 1, 4, 5, 2, 3, 6, 7):
                src, p0 = "BE" if k % 2 == 0 else "BO", 32 * (k // 2)
                mm(A("B%d" % banks[k // 4], 128 * (k % 4), 128 * (k % 4) + 128), A(src, a0, a0 + 128, 1, p0, p0 + 32), A(src, b0, b0 + 128, 1, p0, p0 + 32))
            for i in range(2):
                o, b = A(out, 512 * i, 512 * i + 512), A("B%d" % banks[i])
                if out == "QX":
                    act(o, b, AF.Relu, bias=-13.0)
                else:
                    tt(o, b, A("cth"), OP.is_ge)
        for k in range(8):
            mm(A("B7", 16 * k, 16 * k + 16), A("QA", 128 * k, 128 * k + 128), A("cw0"))
        for k in range(8):
            o = A("B4", 16 * k, 16 * k + 16)
            mm(o, A("QX", 128 * k, 128 * k + 128), A("cw0"), True, False)
            mm(o, A("QB", 128 * k, 128 * k + 128), A("cw1"), False, True)
        for h, b in ((0, "B7"), (1, "B4")):
            tt(A("LT_%d" % h), A(b, 0, 128), A("cmk"), OP.mult)
        for h in range(2):
            mm(A("B0", 8 * h, 8 * h + 8), A("LT_%d" % h), A("cg"), f32=True)
        v = A("B0", 0, 16)
        ts(A("Y1"), v, 256.0, None, OP.is_ge)
        ts(A("Y2"), v, 512.0, None, OP.is_lt)
        tt(A("DD"), v, A("cb2"), OP.subtract)
        tt(A("SEC"), A("Y1"), A("Y2"), OP.mult)
        tt(A("DS"), A("DD"), A("SEC"), OP.mult)
        tt(A("LF"), A("DS"), A("cba"), OP.add)
        copy(A("LU"), A("LF"))
        ts(A("EE"), A("SEC"), -256.0, 256.0, OP.mult, OP.add)
        tt(A("LSF"), A("LF"), A("EE"), OP.add)
        copy(A("LSU"), A("LSF"))
        copy(A("Q"), IND(A("P", 0, 256), A("LU")))
        ne, cn, pn, nc = A("B2", 0, 256), A("B1", 0, 256), A("B6", 0, 256), A("B5", 0, 256)
        tt(ne, ps, A("Q"), OP.not_equal)
        tt(A("MN"), ps, A("Q"), OP.min)
        tt(A("SP"), A("S"), ps, OP.subtract)
        tt(A("QN"), ne, A("MN"), OP.mult)
        ts(A("ND"), A("QN"), 0.0, None, OP.is_le)
        mm(cn, A("cblb"), A("ND"))
        tt(A("SN"), IND(A("cio"), A("LU")), A("ci2"), OP.not_equal)
        tt(A("SPS"), A("SP"), A("SN"), OP.mult)
        tt(pn, ps, A("ND"), OP.mult)
        tt(A("QN"), A("Q"), A("ND"), OP.mult)
        ts(nc, cn, 15.5, None, OP.is_ge)
        tt(A("SX"), A("SPS"), nc, OP.mult)
        tt(A("PC"), A("P", 0, 256), nc, OP.mult)
        tt(A("P", 0, 256), A("SX"), pn, OP.add)
        tt(IND(A("P"), A("LSU")), A("QN"), A("PC"), OP.max)

    for t in range(4):
        for h in range(2):
            middle(h, t)
            hash_(h, 0, t)
            ts(A("PK_%d" % h), A("P", 128 * h, 128 * h + 128), A("ntx", t, t + 1), None, OP.mult)
            look(h, t)
        for p in range(3):
            for h in range(2):
                winner(h, p)
                if p < 2:
                    hash_(h, p + 1, t)
                    look(h, t)
                else:
                    names(h, t)
        pairs(t)
    ts(A("YO"), A("P", 0, 256), -1.0, None, OP.add)

    for o in schedule(ops):
        o[3]()
    order("y", A("YO")[1], [])
    g.sync.dma_start(T.yp[:], T.YO[:]).then_inc(T.sem.dyp, 16)
    need("y", "dyp", 16)
    g.wait_ge(T.sem.loc, tot_loc[0])
    for q in ("v", "s", "t", "g"):
        need("y", qsem[q], cnt[q])
